import numpy as np
import ml_dtypes


def mxq(x, axis, fmt="e4m3"):
    dtype, down = {"e4m3": (ml_dtypes.float8_e4m3fn, 7), "e5m2": (ml_dtypes.float8_e5m2, 14)}[fmt]
    v = np.moveaxis(np.asarray(x, np.float32).astype(ml_dtypes.bfloat16).astype(np.float64), axis, -1)
    blocks = v.reshape(v.shape[:-1] + (-1, 32))
    amax = np.abs(blocks).max(-1, keepdims=True)
    byte = np.maximum(np.where(amax > 0, np.frexp(amax)[1] - 1 + 127, 0) - down, 1)
    scale = np.exp2(byte - 127.0)
    codes = (blocks / scale).astype(np.float32).astype(dtype).astype(np.float64)
    return np.moveaxis((codes * scale).reshape(v.shape), -1, axis)


WIDE = False


def mx_kscale(k):
    if not WIDE:
        return np.ones(k)
    levels = np.array([10, -10, 5, -5, 0])
    if k % 512:
        return np.exp2(np.random.permutation(np.resize(levels, k // 32))).repeat(32)
    a = np.empty((k // 512, 16))
    for p in range(k // 512):
        a[p, :8] = np.random.permutation(np.resize(levels, 8))
        for g in range(8):
            far = levels[np.abs(levels - a[p, g]) >= 10]
            a[p, g + 8] = far[np.random.randint(len(far))]
    return np.exp2(a.ravel()).repeat(32)


def f64(x):
    return np.asarray(x).astype(np.float64)


def striped(idx):
    return np.tile(idx.reshape(-1, 16).T, (8, 1)).astype(np.uint16)


def unstriped(offs):
    return offs[:16].T.reshape(-1).astype(np.int64)


E2M1 = np.array([0.0, 0.5, 1.0, 1.5, 2.0, 3.0, 4.0, 6.0, -0.0, -0.5, -1.0, -1.5, -2.0, -3.0, -4.0, -6.0])


def pack_weight(w, fmt):
    k, n = w.shape
    w = f64(np.asarray(w, np.float32).astype(ml_dtypes.bfloat16)).reshape(k // 32, 32, n)
    amax = np.abs(w).max(1)
    if fmt == "e4m3":
        byte = np.frexp(amax)[1] - 1 + 127 - 7
    else:
        mant, ex = np.frexp(amax / 6.0)
        byte = np.where(mant > 0.5, ex, ex - 1) + 127
    byte = np.clip(np.where(amax > 0, byte, 1), 1, 254)
    scaled = (w * np.exp2(127.0 - byte)[:, None, :]).reshape(k, n).astype(np.float32)
    by_word = np.ascontiguousarray(scaled.reshape(k // 512, 128, 4, n).transpose(0, 1, 3, 2))
    if fmt == "e4m3":
        words = by_word.astype(ml_dtypes.float8_e4m3fn).view(np.uint8)
    else:
        c = by_word.astype(ml_dtypes.float4_e2m1fn).view(np.uint8) & 0xF
        words = (c[..., 0::2] | (c[..., 1::2] << 4)).reshape(k // 512, 128, 2 * n)
    return np.ascontiguousarray(words), np.ascontiguousarray(byte.astype(np.uint8).reshape(k // 512, 16, n))


def unpack_weight(words, scales, fmt):
    g, _, n = scales.shape
    words = np.ascontiguousarray(words).reshape(g, 128, n, -1)
    if fmt == "e4m3":
        vals = words.view(ml_dtypes.float8_e4m3fn).astype(np.float64)
    else:
        nib = np.empty((g, 128, n, 4), np.uint8)
        nib[..., 0::2] = words & 0xF
        nib[..., 1::2] = words >> 4
        vals = E2M1[nib]
    vals = vals * np.repeat(np.exp2(scales.astype(np.float64) - 127.0), 8, axis=1)[..., None]
    return vals.transpose(0, 1, 3, 2).reshape(g * 512, n)


def gelu(v):
    return 0.5 * v * (1.0 + np.tanh(np.sqrt(2.0 / np.pi) * (v + 0.044715 * v**3)))


def bf(x):
    return np.asarray(x, np.float32).astype(ml_dtypes.bfloat16)


def planes(Y):
    n, m = Y.shape
    b = f64(bf(Y)).reshape(n // 32, 32, m)
    amax = np.abs(b).max(1)
    byte = np.clip(np.where(amax > 0, np.frexp(amax)[1] - 1 + 127 - 7, 1), 1, 254)
    codes = (b * np.exp2(127.0 - byte)[:, None, :]).reshape(n, m).astype(np.float32).astype(ml_dtypes.float8_e4m3fn).view(np.uint8)
    words = codes.reshape(n // 512, 128, 4, m).transpose(0, 1, 3, 2)
    return np.ascontiguousarray(words), np.ascontiguousarray(byte.astype(np.uint8).reshape(n // 512, 16, m))


K, T, S, K2, H, N = 1024, 4096, 1024, 512, 1024, 512

def setup_inputs():
    n = np.random.standard_normal
    s = mx_kscale(K)[:, None]
    s2 = mx_kscale(K2)[:, None]
    u = mx_kscale(H)[:, None]
    d = {}
    d["tab_words"], d["tab_scales"] = pack_weight(n((K, T)) * s, "e4m3")
    d["offs"] = striped(np.random.permutation(T)[:S])
    d["xs_words"], d["xs_scales"] = pack_weight(n((K2, S)) * s2, "e4m3")
    d["w1"] = (n((K, H)) / K**0.5 / s * u.T).astype(np.float32)
    d["b1"] = (0.6 * n(H) * u[:, 0]).astype(np.float32)
    d["wa_words"], d["wa_scales"] = pack_weight(n((K2, H)) / K2**0.5 / s2 * u.T, "e2m1")
    d["wb"] = (n((K2, H)) / K2**0.5 / s2 * u.T).astype(np.float32)
    size = np.exp(0.8 * n(N))[None, :]
    d["w2_words"], d["w2_scales"] = pack_weight(n((H, N)) / H**0.5 / u * size, "e4m3")
    return d

def reference(tab_words, tab_scales, offs, xs_words, xs_scales, w1, b1, wa_words, wa_scales, wb, w2_words, w2_scales):
    v = unpack_weight(tab_words, tab_scales, "e4m3")[:, unstriped(offs)]
    xs = unpack_weight(xs_words, xs_scales, "e4m3")
    wa = unpack_weight(wa_words, wa_scales, "e2m1")
    w2 = unpack_weight(w2_words, w2_scales, "e4m3")
    a = (mxq(f64(w1), 0, "e4m3").T @ v) + f64(b1)[:, None]
    b = wa.T @ xs
    e = mxq(f64(wb), 0, "e4m3").T @ xs
    h = np.maximum(a, b) + e
    hq = mxq(h, 0, "e4m3")
    y = w2.T @ hq
    words, scales = planes(y)
    return y, words, scales

@@ -1,0 +1,279 @@
+from contextlib import ExitStack
+
+import concourse.mybir as mybir
+
+K, T, S, K2, H, N = 1024, 4096, 1024, 512, 1024, 512
+FLOPS = 2 * S * (K * H + 2 * K2 * H + H * N)
+
+F32 = mybir.dt.float32
+BF16 = mybir.dt.bfloat16
+I32 = mybir.dt.int32
+U32 = mybir.dt.uint32
+U16 = mybir.dt.uint16
+U8 = mybir.dt.uint8
+FP8X4 = mybir.dt.float8_e4m3fn_x4
+FP4X4 = mybir.dt.float4_e2m1fn_x4
+ADD = mybir.AluOpType.add
+MAX = mybir.AluOpType.max
+
+P = 128
+PACK = 4
+PASS = P * PACK
+CH = 512
+NCH = S // CH
+HB = H // PASS
+KP = K // PASS
+
+
+def tile_list_groove_fill_features_kernel(
+    tc, tab_words, tab_scales, offs, xs_words, xs_scales, w1, b1, wa_words, wa_scales, wb,
+    w2_words, w2_scales, out_0, out_1, out_2,
+):
+    nc = tc.nc
+    with ExitStack() as ctx:
+        keep = ctx.enter_context(tc.tile_pool(name="keep", bufs=1))
+        ring = ctx.enter_context(tc.tile_pool(name="ring", bufs=4))
+        psum = ctx.enter_context(tc.psum_pool(name="psum", bufs=8))
+
+        def held(shape, dtype, name):
+            return keep.tile(shape, dtype, name=name, align_bytes=64)
+
+        def as_words(dram):
+            return dram.rearrange("p n t -> p (n t)").bitcast(I32)
+
+        offsets = keep.tile([P, S // 16], U16, name="offsets")
+        tab_sc = held([P, T], U8, "tab_sc")
+        xs_sc = held([P, S], U8, "xs_sc")
+        wa_sc_raw = held([P, H], U8, "wa_sc_raw")
+        w2_sc_raw = held([P, N], U8, "w2_sc_raw")
+        for plane in (tab_sc, wa_sc_raw, xs_sc, w2_sc_raw):
+            nc.vector.memset(plane[:].bitcast(I32), 0)
+
+        xs_w = held([P, S], I32, "xs_w")
+        nc.sync.dma_start(xs_w[:], as_words(xs_words[0]))
+        wa_raw = held([P, 2 * H], U8, "wa_raw")
+        nc.sync.dma_start(wa_raw[:].bitcast(I32), wa_words[0].bitcast(I32))
+        nc.sync.dma_start(offsets[:], offs)
+        xs_sc_rows = held([P, S // 4], I32, "xs_sc_rows")
+        for q in range(4):
+            rows = slice(4 * q, 4 * q + 4)
+            live = slice(32 * q, 32 * q + 4)
+            nc.sync.dma_start(xs_sc_rows[live, :], xs_scales[0, rows, :].bitcast(I32))
+            nc.vector.tensor_copy(xs_sc[live, :].bitcast(I32), xs_sc_rows[live, :])
+        for q in range(4):
+            rows = slice(4 * q, 4 * q + 4)
+            nc.scalar.dma_start(wa_sc_raw[32 * q : 32 * q + 4, :].bitcast(I32), wa_scales[0, rows, :].bitcast(I32))
+        for q in range(4):
+            rows = slice(4 * q, 4 * q + 4)
+            nc.gpsimd.dma_start(tab_sc[32 * q : 32 * q + 8, :].bitcast(I32), tab_scales[:, rows, :].bitcast(I32))
+        bias = held([P, HB, PACK], F32, "bias")
+        nc.gpsimd.dma_start(bias[:], b1.rearrange("(b p t) -> p b t", p=P, t=PACK))
+        for q in range(4):
+            rows = slice(4 * q, 4 * q + 4)
+            nc.gpsimd.dma_start(w2_sc_raw[32 * q : 32 * q + 8, :].bitcast(I32), w2_scales[:, rows, :].bitcast(I32))
+
+        tab_w = [held([P, T], I32, f"tab_w{a}") for a in range(KP)]
+        for a in range(KP):
+            nc.sync.dma_start(tab_w[a][:], as_words(tab_words[a]))
+
+        def load_weight(w, a, b, name):
+            raw = held([P, PACK, PASS], F32, name)
+            rows = w[a * PASS : (a + 1) * PASS, b * PASS : (b + 1) * PASS]
+            nc.sync.dma_start(raw[:], rows.rearrange("(p j) c -> p j c", j=PACK))
+            return raw
+
+        w1_raw, wb_raw = {}, {}
+        for b in range(HB):
+            for a in range(KP):
+                w1_raw[a, b] = load_weight(w1, a, b, f"w1_raw{a}{b}")
+            wb_raw[b] = load_weight(wb, 0, b, f"wb_raw{b}")
+        w2_raw = held([P, HB, N], I32, "w2_raw")
+        nc.sync.dma_start(w2_raw[:], w2_words.rearrange("a p n t -> p a (n t)").bitcast(I32))
+
+        wa_w = held([P, 2 * H], U8, "wa_w")
+        wa_sc = held([P, H], U8, "wa_sc")
+        nc.vector.tensor_copy(
+            wa_w[:].bitcast(U16).rearrange("p (b t m) -> p b t m", b=HB, t=PACK),
+            wa_raw[:].bitcast(U16).rearrange("p (b m t) -> p b t m", b=HB, t=PACK),
+        )
+        nc.vector.tensor_copy(
+            wa_sc[:].rearrange("p (b t m) -> p b t m", b=HB, t=PACK),
+            wa_sc_raw[:].rearrange("p (b m t) -> p b t m", b=HB, t=PACK),
+        )
+
+        def cols(c):
+            return slice(c * CH, (c + 1) * CH)
+
+        def row_bank():
+            return psum.tile([P, CH], F32, name="bank", tag="bank")
+
+        def quad_bank():
+            return psum.tile([P, PACK, P], F32, name="bank", tag="bank")
+
+        top = {}
+        for b in range(HB):
+            for c in range(NCH):
+                top[b, c] = held([P, PACK, CH], F32, f"top{b}{c}")
+                for t in range(PACK):
+                    bank = row_bank()
+                    r0 = b * PASS + t * P
+                    nc.tensor.matmul_mx(
+                        bank[:],
+                        lhsT=wa_w[:, 2 * r0 : 2 * (r0 + P)].bitcast(FP4X4),
+                        lhsT_scale=wa_sc[:, r0 : r0 + P],
+                        rhs=xs_w[:, cols(c)].bitcast(FP8X4),
+                        rhs_scale=xs_sc[:, cols(c)],
+                        start=True, stop=True,
+                    )
+                    nc.scalar.copy(top[b, c][:, t, :], bank[:])
+
+        v_sc = held([P, S], U8, "v_sc")
+        nc.vector.tensor_copy(v_sc[:], tab_sc[:].indirect(offsets[:]))
+        w2_sc = held([P, N], U8, "w2_sc")
+        nc.gpsimd.tensor_copy(
+            w2_sc[:].rearrange("p (t m) -> p t m", t=PACK),
+            w2_sc_raw[:].rearrange("p (m t) -> p t m", t=PACK),
+        )
+        v_w = [held([P, S], U32, f"v_w{a}") for a in range(KP)]
+        for a in range(KP):
+            nc.vector.tensor_copy(v_w[a][:], tab_w[a][:].bitcast(U32).indirect(offsets[:]))
+
+        def prepare(raw, name, copies):
+            parts = len(copies)
+            width = PASS // parts
+            dealt = raw[:].rearrange("p j (m u v) -> p u m j v", u=2, v=2)
+            rounded = []
+            for i, copy in enumerate(copies):
+                tile = ring.tile([P, PACK * width], BF16, name="w_bf", align_bytes=64)
+                us = slice(i * 2 // parts, (i + 1) * 2 // parts)
+                copy(tile[:].rearrange("p (u v m j) -> p u m j v", v=2, m=P, j=PACK), dealt[:, us, :, :, :])
+                rounded.append(tile)
+            slices = []
+            for i, tile in enumerate(rounded):
+                codes = held([P, width], U32, f"{name}{i}_w")
+                scales = held([P, width], U8, f"{name}{i}_sc")
+                nc.vector.quantize_mx(codes[:].bitcast(FP8X4), scales[:], tile[:])
+                for m0 in range(0, width, P):
+                    slices.append((codes[:, m0 : m0 + P].bitcast(FP8X4), scales[:, m0 : m0 + P]))
+            return slices
+
+        vec, act = nc.vector.tensor_copy, nc.scalar.copy
+        w1_q, wb_q = {}, {}
+
+        def stage_max(b, c):
+            for t in range(PACK):
+                bank = row_bank()
+                for a in range(KP):
+                    codes, scales = w1_q[a, b][t]
+                    nc.tensor.matmul_mx(
+                        bank[:],
+                        lhsT=codes,
+                        lhsT_scale=scales,
+                        rhs=v_w[a][:, cols(c)].bitcast(FP8X4),
+                        rhs_scale=v_sc[4 * a : P, cols(c)],
+                        start=(a == 0), stop=(a == KP - 1),
+                    )
+                nc.vector.scalar_tensor_tensor(
+                    top[b, c][:, t, :], bank[:], bias[:, b, t : t + 1], top[b, c][:, t, :], ADD, MAX
+                )
+
+        def stage_add(b, s0, width):
+            rounded = ring.tile([P, PACK * width], BF16, name="h_bf", align_bytes=64)
+            for g in range(width // P):
+                tok = slice(s0 + g * P, s0 + (g + 1) * P)
+                c, at = divmod(tok.start, CH)
+                bank = quad_bank()
+                for t in range(PACK):
+                    codes, scales = wb_q[b][t]
+                    nc.tensor.matmul_mx(
+                        bank[:, t, :],
+                        lhsT=codes,
+                        lhsT_scale=scales,
+                        rhs=xs_w[:, tok].bitcast(FP8X4),
+                        rhs_scale=xs_sc[:, tok],
+                        start=True, stop=True,
+                    )
+                nc.vector.tensor_tensor(
+                    rounded[:, g * PASS : (g + 1) * PASS].rearrange("p (n i t) -> p n t i", i=2, t=PACK),
+                    bank[:].rearrange("p t (n i) -> p n t i", i=2),
+                    top[b, c][:, :, at : at + P].rearrange("p t (n i) -> p n t i", i=2),
+                    ADD,
+                )
+            return rounded
+
+        w2_w = held([P, HB, N], I32, "w2_w")
+        h_w = [held([P, S], U32, f"h_w{b}") for b in range(HB)]
+        h_sc = [held([P, S], U8, f"h_sc{b}") for b in range(HB)]
+        y_w = held([P, S], U32, "y_w")
+        y_sc = held([P, S], U8, "y_sc")
+        y_rows = out_0.rearrange("(p t) s -> p t s", t=PACK)
+
+        def quantise_h(b, s0, width, rounded):
+            tok = slice(s0, s0 + width)
+            nc.vector.quantize_mx(h_w[b][:, tok].bitcast(FP8X4), h_sc[b][:, tok], rounded[:])
+
+        def stage_y(s0, width, copy):
+            y = ring.tile([P, PACK, width], F32, name="y", align_bytes=64)
+            rounded = ring.tile([P, PACK * width], BF16, name="y_bf", align_bytes=64)
+            for g in range(width // P):
+                tok = slice(s0 + g * P, s0 + (g + 1) * P)
+                bank = quad_bank()
+                for b in range(HB):
+                    for t in range(PACK):
+                        nc.tensor.matmul_mx(
+                            bank[:, t, :],
+                            lhsT=w2_w[:, b, t * P : (t + 1) * P].bitcast(FP8X4),
+                            lhsT_scale=w2_sc[4 * b : P, t * P : (t + 1) * P],
+                            rhs=h_w[b][:, tok].bitcast(FP8X4),
+                            rhs_scale=h_sc[b][:, tok],
+                            start=(b == 0 and t == 0), stop=(b == HB - 1 and t == PACK - 1),
+                        )
+                copy(
+                    rounded[:, g * PASS : (g + 1) * PASS].rearrange("p (n i t) -> p n t i", i=2, t=PACK),
+                    bank[:].rearrange("p t (n i) -> p n t i", i=2),
+                )
+                nc.scalar.copy(y[:, :, g * P : (g + 1) * P], bank[:])
+            nc.sync.dma_start(y_rows[:, :, s0 : s0 + width], y[:])
+            return rounded
+
+        def planes_y(s0, width, rounded):
+            tok = slice(s0, s0 + width)
+            nc.vector.quantize_mx(y_w[:, tok].bitcast(FP8X4), y_sc[:, tok], rounded[:])
+            nc.sync.dma_start(as_words(out_1[0])[:, tok], y_w[:, tok].bitcast(I32))
+
+        w1_q[0, 0] = prepare(w1_raw[0, 0], "w1q00", (vec,))
+        w1_q[1, 0] = prepare(w1_raw[1, 0], "w1q10", (vec, act))
+        stage_max(0, 0)
+        stage_max(0, 1)
+        wb_q[0] = prepare(wb_raw[0], "wbq0", (act,))
+        h_bf = {}
+        h_bf[0, 0] = stage_add(0, 0, CH)
+        w1_q[0, 1] = prepare(w1_raw[0, 1], "w1q01", (act,))
+        h_bf[0, 1] = stage_add(0, CH, CH)
+        quantise_h(0, 0, CH, h_bf[0, 0])
+        w1_q[1, 1] = prepare(w1_raw[1, 1], "w1q11", (act,))
+        nc.gpsimd.tensor_copy(
+            w2_w[:].rearrange("p a (t m) -> p a m t", t=PACK),
+            w2_raw[:].rearrange("p a (m t) -> p a m t", t=PACK),
+        )
+        stage_max(1, 0)
+        quantise_h(0, CH, CH, h_bf[0, 1])
+        wb_q[1] = prepare(wb_raw[1], "wbq1", (act,))
+        wide = 2 * P
+        pieces = [(s0, wide) for s0 in range(0, S - wide, wide)] + [(S - wide, P), (S - P, P)]
+        y_bf = {}
+        for i in range(len(pieces) + 2):
+            if i == CH // wide:
+                stage_max(1, 1)
+            if i >= 2:
+                planes_y(*pieces[i - 2], y_bf[i - 2])
+            if i < len(pieces):
+                h_bf[1, i] = stage_add(1, *pieces[i])
+            if 1 <= i <= len(pieces):
+                quantise_h(1, *pieces[i - 1], h_bf[1, i - 1])
+                y_bf[i - 1] = stage_y(*pieces[i - 1], vec if pieces[i - 1][1] == P else act)
+        for q in range(4):
+            queue = nc.scalar if q % 2 else nc.sync
+            queue.dma_start(
+                out_2[0, 4 * q : 4 * q + 4, :].bitcast(I32), y_sc[32 * q : 32 * q + 4, :].bitcast(I32)
+            )

@@ -46,47 +46,55 @@ def tile_list_groove_fill_features_kernel(
         xs_sc = held([P, S], U8, "xs_sc")
         wa_sc_raw = held([P, H], U8, "wa_sc_raw")
         w2_sc_raw = held([P, N], U8, "w2_sc_raw")
-        for plane in (tab_sc, wa_sc_raw, xs_sc, w2_sc_raw):
+        for plane in (wa_sc_raw, xs_sc, tab_sc, w2_sc_raw):
             nc.vector.memset(plane[:].bitcast(I32), 0)
 
-        xs_w = held([P, S], I32, "xs_w")
-        nc.sync.dma_start(xs_w[:], as_words(xs_words[0]))
-        wa_raw = held([P, 2 * H], U8, "wa_raw")
-        nc.sync.dma_start(wa_raw[:].bitcast(I32), wa_words[0].bitcast(I32))
-        nc.sync.dma_start(offsets[:], offs)
-        xs_sc_rows = held([P, S // 4], I32, "xs_sc_rows")
-        for q in range(4):
-            rows = slice(4 * q, 4 * q + 4)
-            live = slice(32 * q, 32 * q + 4)
-            nc.sync.dma_start(xs_sc_rows[live, :], xs_scales[0, rows, :].bitcast(I32))
-            nc.vector.tensor_copy(xs_sc[live, :].bitcast(I32), xs_sc_rows[live, :])
-        for q in range(4):
-            rows = slice(4 * q, 4 * q + 4)
-            nc.scalar.dma_start(wa_sc_raw[32 * q : 32 * q + 4, :].bitcast(I32), wa_scales[0, rows, :].bitcast(I32))
-        for q in range(4):
-            rows = slice(4 * q, 4 * q + 4)
-            nc.gpsimd.dma_start(tab_sc[32 * q : 32 * q + 8, :].bitcast(I32), tab_scales[:, rows, :].bitcast(I32))
-        bias = held([P, HB, PACK], F32, "bias")
-        nc.gpsimd.dma_start(bias[:], b1.rearrange("(b p t) -> p b t", p=P, t=PACK))
-        for q in range(4):
-            rows = slice(4 * q, 4 * q + 4)
-            nc.gpsimd.dma_start(w2_sc_raw[32 * q : 32 * q + 8, :].bitcast(I32), w2_scales[:, rows, :].bitcast(I32))
-
-        tab_w = [held([P, T], I32, f"tab_w{a}") for a in range(KP)]
-        for a in range(KP):
-            nc.sync.dma_start(tab_w[a][:], as_words(tab_words[a]))
+        def load_scale_rows(plane, dram, first, rs):
+            for r in rs:
+                nc.sync.dma_start(plane[first + r : P : 32, :], dram[r:16:4, :].bitcast(I32))
 
         def load_weight(w, a, b, name):
             raw = held([P, PACK, PASS], F32, name)
             rows = w[a * PASS : (a + 1) * PASS, b * PASS : (b + 1) * PASS]
             nc.sync.dma_start(raw[:], rows.rearrange("(p j) c -> p j c", j=PACK))
             return raw
+        tab_w = [held([P, T], I32, f"tab_w{a}") for a in range(KP)]
 
+        def load_table(a, half):
+            part = slice(half * T // 2, (half + 1) * T // 2)
+            nc.sync.dma_start(tab_w[a][:, part], as_words(tab_words[a])[:, part])
+
+        xs_w = held([P, S], I32, "xs_w")
+        nc.sync.dma_start(xs_w[:], as_words(xs_words[0]))
+        wa_raw = held([P, 2 * H], U8, "wa_raw")
+        nc.sync.dma_start(wa_raw[:].bitcast(I32), wa_words[0].bitcast(I32))
+        xs_sc_rows = held([P, S // 4], I32, "xs_sc_rows")
+        for q in range(4):
+            live = slice(32 * q, 32 * q + 4)
+            nc.sync.dma_start(xs_sc_rows[live, :], xs_scales[0, 4 * q : 4 * q + 4, :].bitcast(I32))
+            nc.vector.tensor_copy(xs_sc[live, :].bitcast(I32), xs_sc_rows[live, :])
+        nc.sync.dma_start(offsets[:], offs)
+        load_table(0, 0)
+        load_scale_rows(wa_sc_raw[:].bitcast(I32), wa_scales[0], 0, range(4))
+        load_table(0, 1)
+        load_scale_rows(tab_sc[:].bitcast(I32), tab_scales[0], 0, range(2))
+        load_table(1, 0)
+        load_scale_rows(tab_sc[:].bitcast(I32), tab_scales[0], 0, range(2, 4))
+        load_scale_rows(tab_sc[:].bitcast(I32), tab_scales[1], 4, range(4))
+        load_table(1, 1)
         w1_raw, wb_raw = {}, {}
-        for b in range(HB):
-            for a in range(KP):
-                w1_raw[a, b] = load_weight(w1, a, b, f"w1_raw{a}{b}")
-            wb_raw[b] = load_weight(wb, 0, b, f"wb_raw{b}")
+        w1_raw[0, 0] = load_weight(w1, 0, 0, "w1_raw00")
+        w1_raw[1, 0] = load_weight(w1, 1, 0, "w1_raw10")
+        bias = held([P, HB, PACK], F32, "bias")
+        nc.sync.dma_start(bias[:], b1.rearrange("(b p t) -> p b t", p=P, t=PACK))
+        wb_raw[0] = load_weight(wb, 0, 0, "wb_raw0")
+        for q in range(4):
+            nc.sync.dma_start(
+                w2_sc_raw[32 * q : 32 * q + 8, :].bitcast(I32), w2_scales[:, 4 * q : 4 * q + 4, :].bitcast(I32)
+            )
+        w1_raw[0, 1] = load_weight(w1, 0, 1, "w1_raw01")
+        w1_raw[1, 1] = load_weight(w1, 1, 1, "w1_raw11")
+        wb_raw[1] = load_weight(wb, 0, 1, "wb_raw1")
         w2_raw = held([P, HB, N], I32, "w2_raw")
         nc.sync.dma_start(w2_raw[:], w2_words.rearrange("a p n t -> p a (n t)").bitcast(I32))
 
@@ -111,7 +119,8 @@ def tile_list_groove_fill_features_kernel(
             return psum.tile([P, PACK, P], F32, name="bank", tag="bank")
 
         top = {}
-        for b in range(HB):
+
+        def stage_b(b):
             for c in range(NCH):
                 top[b, c] = held([P, PACK, CH], F32, f"top{b}{c}")
                 for t in range(PACK):
@@ -127,13 +136,9 @@ def tile_list_groove_fill_features_kernel(
                     )
                     nc.scalar.copy(top[b, c][:, t, :], bank[:])
 
+        stage_b(0)
         v_sc = held([P, S], U8, "v_sc")
         nc.vector.tensor_copy(v_sc[:], tab_sc[:].indirect(offsets[:]))
-        w2_sc = held([P, N], U8, "w2_sc")
-        nc.gpsimd.tensor_copy(
-            w2_sc[:].rearrange("p (t m) -> p t m", t=PACK),
-            w2_sc_raw[:].rearrange("p (m t) -> p t m", t=PACK),
-        )
         v_w = [held([P, S], U32, f"v_w{a}") for a in range(KP)]
         for a in range(KP):
             nc.vector.tensor_copy(v_w[a][:], tab_w[a][:].bitcast(U32).indirect(offsets[:]))
@@ -243,35 +248,50 @@ def tile_list_groove_fill_features_kernel(
 
         w1_q[0, 0] = prepare(w1_raw[0, 0], "w1q00", (vec,))
         w1_q[1, 0] = prepare(w1_raw[1, 0], "w1q10", (vec, act))
+        stage_b(1)
         stage_max(0, 0)
         stage_max(0, 1)
         wb_q[0] = prepare(wb_raw[0], "wbq0", (act,))
         h_bf = {}
         h_bf[0, 0] = stage_add(0, 0, CH)
         w1_q[0, 1] = prepare(w1_raw[0, 1], "w1q01", (act,))
-        h_bf[0, 1] = stage_add(0, CH, CH)
-        quantise_h(0, 0, CH, h_bf[0, 0])
         w1_q[1, 1] = prepare(w1_raw[1, 1], "w1q11", (act,))
-        nc.gpsimd.tensor_copy(
-            w2_w[:].rearrange("p a (t m) -> p a m t", t=PACK),
-            w2_raw[:].rearrange("p a (m t) -> p a m t", t=PACK),
-        )
+        quantise_h(0, 0, CH, h_bf[0, 0])
         stage_max(1, 0)
-        quantise_h(0, CH, CH, h_bf[0, 1])
         wb_q[1] = prepare(wb_raw[1], "wbq1", (act,))
+        w2_sc = held([P, N], U8, "w2_sc")
+        nc.vector.tensor_copy(
+            w2_sc[:].rearrange("p (t m) -> p t m", t=PACK),
+            w2_sc_raw[:].rearrange("p (m t) -> p t m", t=PACK),
+        )
+        nc.vector.tensor_copy(
+            w2_w[:].rearrange("p a (u v m) -> p a u m v", u=2, v=2),
+            w2_raw[:].rearrange("p a (m u v) -> p a u m v", u=2, v=2),
+        )
         wide = 2 * P
         pieces = [(s0, wide) for s0 in range(0, S - wide, wide)] + [(S - wide, P), (S - P, P)]
         y_bf = {}
-        for i in range(len(pieces) + 2):
-            if i == CH // wide:
-                stage_max(1, 1)
-            if i >= 2:
-                planes_y(*pieces[i - 2], y_bf[i - 2])
-            if i < len(pieces):
-                h_bf[1, i] = stage_add(1, *pieces[i])
-            if 1 <= i <= len(pieces):
-                quantise_h(1, *pieces[i - 1], h_bf[1, i - 1])
-                y_bf[i - 1] = stage_y(*pieces[i - 1], vec if pieces[i - 1][1] == P else act)
+        first, second = pieces[:2], pieces[2:]
+        for piece in first:
+            h_bf[1, piece] = stage_add(1, *piece)
+        for piece in first:
+            quantise_h(1, *piece, h_bf[1, piece])
+        for piece in first:
+            y_bf[piece] = stage_y(*piece, act)
+        h_bf[0, 1] = stage_add(0, CH, CH)
+        planes_y(*first[0], y_bf[first[0]])
+        stage_max(1, 1)
+        quantise_h(0, CH, CH, h_bf[0, 1])
+        planes_y(*first[1], y_bf[first[1]])
+        for i in range(len(second) + 1):
+            if i < len(second):
+                h_bf[1, second[i]] = stage_add(1, *second[i])
+            if i >= 1:
+                piece = second[i - 1]
+                quantise_h(1, *piece, h_bf[1, piece])
+                y_bf[piece] = stage_y(*piece, vec if piece[1] == P else act)
+        for piece in second:
+            planes_y(*piece, y_bf[piece])
         for q in range(4):
             queue = nc.scalar if q % 2 else nc.sync
             queue.dma_start(

@@ -33,7 +33,7 @@ def tile_list_groove_fill_features_kernel(
     with ExitStack() as ctx:
         keep = ctx.enter_context(tc.tile_pool(name="keep", bufs=1))
         ring = ctx.enter_context(tc.tile_pool(name="ring", bufs=4))
-        psum = ctx.enter_context(tc.psum_pool(name="psum", bufs=8))
+        psum = ctx.enter_context(tc.psum_pool(name="psum", bufs=1))
 
         def held(shape, dtype, name):
             return keep.tile(shape, dtype, name=name, align_bytes=64)
@@ -46,6 +46,7 @@ def tile_list_groove_fill_features_kernel(
         xs_sc = held([P, S], U8, "xs_sc")
         wa_sc_raw = held([P, H], U8, "wa_sc_raw")
         w2_sc_raw = held([P, N], U8, "w2_sc_raw")
+        v_sc = held([P, S], U8, "v_sc")
         for plane in (wa_sc_raw, xs_sc, tab_sc, w2_sc_raw):
             nc.vector.memset(plane[:].bitcast(I32), 0)
 
@@ -69,21 +70,22 @@ def tile_list_groove_fill_features_kernel(
         wa_raw = held([P, 2 * H], U8, "wa_raw")
         nc.sync.dma_start(wa_raw[:].bitcast(I32), wa_words[0].bitcast(I32))
         xs_sc_rows = held([P, S // 4], I32, "xs_sc_rows")
+        load_scale_rows(xs_sc_rows[:], xs_scales[0], 0, range(4))
         for q in range(4):
             live = slice(32 * q, 32 * q + 4)
-            nc.sync.dma_start(xs_sc_rows[live, :], xs_scales[0, 4 * q : 4 * q + 4, :].bitcast(I32))
             nc.vector.tensor_copy(xs_sc[live, :].bitcast(I32), xs_sc_rows[live, :])
         nc.sync.dma_start(offsets[:], offs)
         load_table(0, 0)
         load_scale_rows(wa_sc_raw[:].bitcast(I32), wa_scales[0], 0, range(4))
         load_table(0, 1)
-        load_scale_rows(tab_sc[:].bitcast(I32), tab_scales[0], 0, range(2))
-        load_table(1, 0)
-        load_scale_rows(tab_sc[:].bitcast(I32), tab_scales[0], 0, range(2, 4))
-        load_scale_rows(tab_sc[:].bitcast(I32), tab_scales[1], 4, range(4))
-        load_table(1, 1)
         w1_raw, wb_raw = {}, {}
-        w1_raw[0, 0] = load_weight(w1, 0, 0, "w1_raw00")
+        for r in range(4):
+            for a in range(KP):
+                load_scale_rows(tab_sc[:].bitcast(I32), tab_scales[a], 4 * (a + 1), [r])
+            if r == 0:
+                w1_raw[0, 0] = load_weight(w1, 0, 0, "w1_raw00")
+        load_table(1, 0)
+        load_table(1, 1)
         w1_raw[1, 0] = load_weight(w1, 1, 0, "w1_raw10")
         bias = held([P, HB, PACK], F32, "bias")
         nc.sync.dma_start(bias[:], b1.rearrange("(b p t) -> p b t", p=P, t=PACK))
@@ -112,11 +114,19 @@ def tile_list_groove_fill_features_kernel(
         def cols(c):
             return slice(c * CH, (c + 1) * CH)
 
-        def row_bank():
-            return psum.tile([P, CH], F32, name="bank", tag="bank")
+        taken = {"h": [], "y": []}
+        depth = {"h": 5, "y": 3}
 
-        def quad_bank():
-            return psum.tile([P, PACK, P], F32, name="bank", tag="bank")
+        def next_bank(shape, ring_name):
+            banks = taken[ring_name]
+            banks.append(psum.tile(shape, F32, name=f"{ring_name}_bank{len(banks) % depth[ring_name]}"))
+            return banks[-1]
+
+        def row_bank():
+            return next_bank([P, CH], "h")
+
+        def quad_bank(ring_name):
+            return next_bank([P, PACK, P], ring_name)
 
         top = {}
 
@@ -137,24 +147,23 @@ def tile_list_groove_fill_features_kernel(
                     nc.scalar.copy(top[b, c][:, t, :], bank[:])
 
         stage_b(0)
-        v_sc = held([P, S], U8, "v_sc")
-        nc.vector.tensor_copy(v_sc[:], tab_sc[:].indirect(offsets[:]))
         v_w = [held([P, S], U32, f"v_w{a}") for a in range(KP)]
-        for a in range(KP):
-            nc.vector.tensor_copy(v_w[a][:], tab_w[a][:].bitcast(U32).indirect(offsets[:]))
 
-        def prepare(raw, name, copies):
+        def round_weight(raw, copies):
             parts = len(copies)
-            width = PASS // parts
             dealt = raw[:].rearrange("p j (m u v) -> p u m j v", u=2, v=2)
             rounded = []
             for i, copy in enumerate(copies):
-                tile = ring.tile([P, PACK * width], BF16, name="w_bf", align_bytes=64)
+                tile = ring.tile([P, PACK * PASS // parts], BF16, name="w_bf", align_bytes=64)
                 us = slice(i * 2 // parts, (i + 1) * 2 // parts)
                 copy(tile[:].rearrange("p (u v m j) -> p u m j v", v=2, m=P, j=PACK), dealt[:, us, :, :, :])
                 rounded.append(tile)
+            return rounded
+
+        def quantise_weight(rounded, name):
             slices = []
             for i, tile in enumerate(rounded):
+                width = tile.shape[1] // PACK
                 codes = held([P, width], U32, f"{name}{i}_w")
                 scales = held([P, width], U8, f"{name}{i}_sc")
                 nc.vector.quantize_mx(codes[:].bitcast(FP8X4), scales[:], tile[:])
@@ -165,29 +174,32 @@ def tile_list_groove_fill_features_kernel(
         vec, act = nc.vector.tensor_copy, nc.scalar.copy
         w1_q, wb_q = {}, {}
 
-        def stage_max(b, c):
-            for t in range(PACK):
+        def stage_max(b, s0, width, ts=range(PACK)):
+            tok = slice(s0, s0 + width)
+            c, at = divmod(s0, CH)
+            for t in ts:
                 bank = row_bank()
                 for a in range(KP):
                     codes, scales = w1_q[a, b][t]
                     nc.tensor.matmul_mx(
-                        bank[:],
+                        bank[:, :width],
                         lhsT=codes,
                         lhsT_scale=scales,
-                        rhs=v_w[a][:, cols(c)].bitcast(FP8X4),
-                        rhs_scale=v_sc[4 * a : P, cols(c)],
+                        rhs=v_w[a][:, tok].bitcast(FP8X4),
+                        rhs_scale=v_sc[4 * (a + 1) : P, tok],
                         start=(a == 0), stop=(a == KP - 1),
                     )
-                nc.vector.scalar_tensor_tensor(
-                    top[b, c][:, t, :], bank[:], bias[:, b, t : t + 1], top[b, c][:, t, :], ADD, MAX
-                )
+                kept = top[b, c][:, t, at : at + width]
+                nc.vector.scalar_tensor_tensor(kept, bank[:, :width], bias[:, b, t : t + 1], kept, ADD, MAX)
 
-        def stage_add(b, s0, width):
-            rounded = ring.tile([P, PACK * width], BF16, name="h_bf", align_bytes=64)
-            for g in range(width // P):
+        def h_tile(width):
+            return ring.tile([P, PACK * width], BF16, name="h_bf", align_bytes=64)
+
+        def stage_add(b, s0, rounded, gs):
+            for g in gs:
                 tok = slice(s0 + g * P, s0 + (g + 1) * P)
                 c, at = divmod(tok.start, CH)
-                bank = quad_bank()
+                bank = quad_bank("h")
                 for t in range(PACK):
                     codes, scales = wb_q[b][t]
                     nc.tensor.matmul_mx(
@@ -198,13 +210,14 @@ def tile_list_groove_fill_features_kernel(
                         rhs_scale=xs_sc[:, tok],
                         start=True, stop=True,
                     )
+                kept = top[b, c][:, :, at : at + P]
+                part = rounded[:, g * PASS : (g + 1) * PASS]
                 nc.vector.tensor_tensor(
-                    rounded[:, g * PASS : (g + 1) * PASS].rearrange("p (n i t) -> p n t i", i=2, t=PACK),
+                    part.rearrange("p (n i t) -> p n t i", i=2, t=PACK),
                     bank[:].rearrange("p t (n i) -> p n t i", i=2),
-                    top[b, c][:, :, at : at + P].rearrange("p t (n i) -> p n t i", i=2),
+                    kept.rearrange("p t (n i) -> p n t i", i=2),
                     ADD,
                 )
-            return rounded
 
         w2_w = held([P, HB, N], I32, "w2_w")
         h_w = [held([P, S], U32, f"h_w{b}") for b in range(HB)]
@@ -222,7 +235,7 @@ def tile_list_groove_fill_features_kernel(
             rounded = ring.tile([P, PACK * width], BF16, name="y_bf", align_bytes=64)
             for g in range(width // P):
                 tok = slice(s0 + g * P, s0 + (g + 1) * P)
-                bank = quad_bank()
+                bank = quad_bank("y")
                 for b in range(HB):
                     for t in range(PACK):
                         nc.tensor.matmul_mx(
@@ -246,54 +259,72 @@ def tile_list_groove_fill_features_kernel(
             nc.vector.quantize_mx(y_w[:, tok].bitcast(FP8X4), y_sc[:, tok], rounded[:])
             nc.sync.dma_start(as_words(out_1[0])[:, tok], y_w[:, tok].bitcast(I32))
 
-        w1_q[0, 0] = prepare(w1_raw[0, 0], "w1q00", (vec,))
-        w1_q[1, 0] = prepare(w1_raw[1, 0], "w1q10", (vec, act))
+        nc.vector.tensor_copy(v_w[0][:], tab_w[0][:].bitcast(U32).indirect(offsets[:]))
+        w1_q[0, 0] = quantise_weight(round_weight(w1_raw[0, 0], (vec,)), "w1q00")
+        nc.vector.tensor_copy(v_sc[:], tab_sc[:].indirect(offsets[:]))
+        nc.vector.tensor_copy(v_w[1][:], tab_w[1][:].bitcast(U32).indirect(offsets[:]))
+        w1_q[1, 0] = quantise_weight(round_weight(w1_raw[1, 0], (vec, act)), "w1q10")
         stage_b(1)
-        stage_max(0, 0)
-        stage_max(0, 1)
-        wb_q[0] = prepare(wb_raw[0], "wbq0", (act,))
-        h_bf = {}
-        h_bf[0, 0] = stage_add(0, 0, CH)
-        w1_q[0, 1] = prepare(w1_raw[0, 1], "w1q01", (act,))
-        w1_q[1, 1] = prepare(w1_raw[1, 1], "w1q11", (act,))
-        quantise_h(0, 0, CH, h_bf[0, 0])
-        stage_max(1, 0)
-        wb_q[1] = prepare(wb_raw[1], "wbq1", (act,))
+        stage_max(0, 0, CH)
+        rounded = round_weight(wb_raw[0], (act,))
+        stage_max(0, CH, CH, range(2))
+        wb_q[0] = quantise_weight(rounded, "wbq0")
+        stage_max(0, CH, CH, range(2, 4))
+        rounded = round_weight(w1_raw[0, 1], (act,))
+        h00 = h_tile(CH)
+        stage_add(0, 0, h00, range(2))
+        w1_q[0, 1] = quantise_weight(rounded, "w1q01")
+        rounded = round_weight(w1_raw[1, 1], (act,))
+        stage_add(0, 0, h00, range(2, 4))
+        w1_q[1, 1] = quantise_weight(rounded, "w1q11")
+        quantise_h(0, 0, CH, h00)
+        rounded = round_weight(wb_raw[1], (act,))
+        stage_max(1, 0, CH, range(3))
+        wb_q[1] = quantise_weight(rounded, "wbq1")
+        stage_max(1, 0, CH, range(3, 4))
         w2_sc = held([P, N], U8, "w2_sc")
-        nc.vector.tensor_copy(
+        nc.gpsimd.tensor_copy(
             w2_sc[:].rearrange("p (t m) -> p t m", t=PACK),
             w2_sc_raw[:].rearrange("p (m t) -> p t m", t=PACK),
         )
-        nc.vector.tensor_copy(
-            w2_w[:].rearrange("p a (u v m) -> p a u m v", u=2, v=2),
-            w2_raw[:].rearrange("p a (m u v) -> p a u m v", u=2, v=2),
+        nc.scalar.copy(
+            w2_w[:].bitcast(U32).rearrange("p a (u v m) -> p a u m v", u=2, v=2),
+            w2_raw[:].bitcast(U32).rearrange("p a (m u v) -> p a u m v", u=2, v=2),
         )
         wide = 2 * P
         pieces = [(s0, wide) for s0 in range(0, S - wide, wide)] + [(S - wide, P), (S - P, P)]
-        y_bf = {}
         first, second = pieces[:2], pieces[2:]
+        h_bf, y_bf = {}, {}
+
+        def add_piece(piece):
+            h_bf[piece] = h_tile(piece[1])
+            stage_add(1, piece[0], h_bf[piece], range(piece[1] // P))
+
         for piece in first:
-            h_bf[1, piece] = stage_add(1, *piece)
+            add_piece(piece)
         for piece in first:
-            quantise_h(1, *piece, h_bf[1, piece])
+            quantise_h(1, *piece, h_bf[piece])
         for piece in first:
             y_bf[piece] = stage_y(*piece, act)
-        h_bf[0, 1] = stage_add(0, CH, CH)
+        h01 = h_tile(CH)
+        stage_add(0, CH, h01, range(CH // P))
         planes_y(*first[0], y_bf[first[0]])
-        stage_max(1, 1)
-        quantise_h(0, CH, CH, h_bf[0, 1])
+        stage_max(1, CH, wide)
+        quantise_h(0, CH, CH, h01)
+        add_piece(second[0])
         planes_y(*first[1], y_bf[first[1]])
-        for i in range(len(second) + 1):
-            if i < len(second):
-                h_bf[1, second[i]] = stage_add(1, *second[i])
-            if i >= 1:
-                piece = second[i - 1]
-                quantise_h(1, *piece, h_bf[1, piece])
-                y_bf[piece] = stage_y(*piece, vec if piece[1] == P else act)
-        for piece in second:
+        quantise_h(1, *second[0], h_bf[second[0]])
+        y_bf[second[0]] = stage_y(*second[0], act)
+        stage_max(1, CH + wide, wide)
+        for piece in second[1:]:
+            add_piece(piece)
+        planes_y(*second[0], y_bf[second[0]])
+        for piece in second[1:]:
+            quantise_h(1, *piece, h_bf[piece])
+        y_bf[second[1]] = stage_y(*second[1], act)
+        y_bf[second[2]] = stage_y(*second[2], vec)
+        for piece in second[1:]:
             planes_y(*piece, y_bf[piece])
         for q in range(4):
             queue = nc.scalar if q % 2 else nc.sync
-            queue.dma_start(
-                out_2[0, 4 * q : 4 * q + 4, :].bitcast(I32), y_sc[32 * q : 32 * q + 4, :].bitcast(I32)
-            )
+            queue.dma_start(out_2[0, q:16:4, :].bitcast(I32), y_sc[q:P:32, :].bitcast(I32))

@@ -19,10 +19,12 @@ MAX = mybir.AluOpType.max
 P = 128
 PACK = 4
 PASS = P * PACK
-CH = 512
-NCH = S // CH
-HB = H // PASS
-KP = K // PASS
+K_PASSES = K // PASS
+H_BLOCKS = H // PASS
+HALF = 512
+QUARTER = HALF // 2
+RING_DEPTH = 4
+BANKS = {"h": 5, "y": 3}
 
 
 def tile_list_groove_fill_features_kernel(
@@ -32,11 +34,11 @@ def tile_list_groove_fill_features_kernel(
     nc = tc.nc
     with ExitStack() as ctx:
         keep = ctx.enter_context(tc.tile_pool(name="keep", bufs=1))
-        ring = ctx.enter_context(tc.tile_pool(name="ring", bufs=4))
+        ring = ctx.enter_context(tc.tile_pool(name="ring", bufs=RING_DEPTH))
         psum = ctx.enter_context(tc.psum_pool(name="psum", bufs=1))
 
-        def held(shape, dtype, name):
-            return keep.tile(shape, dtype, name=name, align_bytes=64)
+        def held(shape, dtype, slot):
+            return keep.tile(shape, dtype, name=slot, align_bytes=64)
 
         def as_words(dram):
             return dram.rearrange("p n t -> p (n t)").bitcast(I32)
@@ -45,116 +47,113 @@ def tile_list_groove_fill_features_kernel(
         tab_sc = held([P, T], U8, "tab_sc")
         xs_sc = held([P, S], U8, "xs_sc")
         wa_sc_raw = held([P, H], U8, "wa_sc_raw")
-        w2_sc_raw = held([P, N], U8, "w2_sc_raw")
         v_sc = held([P, S], U8, "v_sc")
-        for plane in (wa_sc_raw, xs_sc, tab_sc, w2_sc_raw):
+        for plane in (wa_sc_raw, tab_sc, xs_sc, v_sc):
             nc.vector.memset(plane[:].bitcast(I32), 0)
 
-        def load_scale_rows(plane, dram, first, rs):
-            for r in rs:
-                nc.sync.dma_start(plane[first + r : P : 32, :], dram[r:16:4, :].bitcast(I32))
+        def load_scale_rows(plane, dram):
+            for r in range(4):
+                nc.sync.dma_start(plane[r:P:32, :], dram[r:16:4, :].bitcast(I32))
 
-        def load_weight(w, a, b, name):
-            raw = held([P, PACK, PASS], F32, name)
+        def load_weight(w, a, b, slot):
+            raw = held([P, PACK, PASS], F32, slot)
             rows = w[a * PASS : (a + 1) * PASS, b * PASS : (b + 1) * PASS]
             nc.sync.dma_start(raw[:], rows.rearrange("(p j) c -> p j c", j=PACK))
             return raw
-        tab_w = [held([P, T], I32, f"tab_w{a}") for a in range(KP)]
 
-        def load_table(a, half):
-            part = slice(half * T // 2, (half + 1) * T // 2)
-            nc.sync.dma_start(tab_w[a][:, part], as_words(tab_words[a])[:, part])
+        tab_w = [held([P, T], I32, f"tab_w{a}") for a in range(K_PASSES)]
+
+        def load_table(a, part):
+            columns = slice(part * T // 2, (part + 1) * T // 2)
+            nc.sync.dma_start(tab_w[a][:, columns], as_words(tab_words[a])[:, columns])
 
         xs_w = held([P, S], I32, "xs_w")
         nc.sync.dma_start(xs_w[:], as_words(xs_words[0]))
         wa_raw = held([P, 2 * H], U8, "wa_raw")
         nc.sync.dma_start(wa_raw[:].bitcast(I32), wa_words[0].bitcast(I32))
         xs_sc_rows = held([P, S // 4], I32, "xs_sc_rows")
-        load_scale_rows(xs_sc_rows[:], xs_scales[0], 0, range(4))
-        for q in range(4):
-            live = slice(32 * q, 32 * q + 4)
+        load_scale_rows(xs_sc_rows[:], xs_scales[0])
+        for quadrant in range(4):
+            live = slice(32 * quadrant, 32 * quadrant + 4)
             nc.vector.tensor_copy(xs_sc[live, :].bitcast(I32), xs_sc_rows[live, :])
         nc.sync.dma_start(offsets[:], offs)
         load_table(0, 0)
-        load_scale_rows(wa_sc_raw[:].bitcast(I32), wa_scales[0], 0, range(4))
+        load_scale_rows(wa_sc_raw[:].bitcast(I32), wa_scales[0])
+        nc.sync.dma_start(tab_sc[0:P:4, :].bitcast(I32), tab_scales.rearrange("a q n -> (a q) n").bitcast(I32))
         load_table(0, 1)
         w1_raw, wb_raw = {}, {}
-        for r in range(4):
-            for a in range(KP):
-                load_scale_rows(tab_sc[:].bitcast(I32), tab_scales[a], 4 * (a + 1), [r])
-            if r == 0:
-                w1_raw[0, 0] = load_weight(w1, 0, 0, "w1_raw00")
+        w1_raw[0, 0] = load_weight(w1, 0, 0, "w1_raw00")
         load_table(1, 0)
         load_table(1, 1)
-        w1_raw[1, 0] = load_weight(w1, 1, 0, "w1_raw10")
-        bias = held([P, HB, PACK], F32, "bias")
+        bias = held([P, H_BLOCKS, PACK], F32, "bias")
         nc.sync.dma_start(bias[:], b1.rearrange("(b p t) -> p b t", p=P, t=PACK))
-        wb_raw[0] = load_weight(wb, 0, 0, "wb_raw0")
-        for q in range(4):
-            nc.sync.dma_start(
-                w2_sc_raw[32 * q : 32 * q + 8, :].bitcast(I32), w2_scales[:, 4 * q : 4 * q + 4, :].bitcast(I32)
-            )
-        w1_raw[0, 1] = load_weight(w1, 0, 1, "w1_raw01")
-        w1_raw[1, 1] = load_weight(w1, 1, 1, "w1_raw11")
-        wb_raw[1] = load_weight(wb, 0, 1, "wb_raw1")
-        w2_raw = held([P, HB, N], I32, "w2_raw")
-        nc.sync.dma_start(w2_raw[:], w2_words.rearrange("a p n t -> p a (n t)").bitcast(I32))
 
         wa_w = held([P, 2 * H], U8, "wa_w")
         wa_sc = held([P, H], U8, "wa_sc")
         nc.vector.tensor_copy(
-            wa_w[:].bitcast(U16).rearrange("p (b t m) -> p b t m", b=HB, t=PACK),
-            wa_raw[:].bitcast(U16).rearrange("p (b m t) -> p b t m", b=HB, t=PACK),
+            wa_w[:].bitcast(U16).rearrange("p (b t m) -> p b t m", b=H_BLOCKS, t=PACK),
+            wa_raw[:].bitcast(U16).rearrange("p (b m t) -> p b t m", b=H_BLOCKS, t=PACK),
         )
         nc.vector.tensor_copy(
-            wa_sc[:].rearrange("p (b t m) -> p b t m", b=HB, t=PACK),
-            wa_sc_raw[:].rearrange("p (b m t) -> p b t m", b=HB, t=PACK),
+            wa_sc[:].rearrange("p (b t m) -> p b t m", b=H_BLOCKS, t=PACK),
+            wa_sc_raw[:].rearrange("p (b m t) -> p b t m", b=H_BLOCKS, t=PACK),
         )
 
-        def cols(c):
-            return slice(c * CH, (c + 1) * CH)
+        banks_taken = {"h": [], "y": []}
 
-        taken = {"h": [], "y": []}
-        depth = {"h": 5, "y": 3}
+        def next_bank(shape, use):
+            taken = banks_taken[use]
+            taken.append(psum.tile(shape, F32, name=f"{use}_bank{len(taken) % BANKS[use]}"))
+            return taken[-1]
 
-        def next_bank(shape, ring_name):
-            banks = taken[ring_name]
-            banks.append(psum.tile(shape, F32, name=f"{ring_name}_bank{len(banks) % depth[ring_name]}"))
-            return banks[-1]
+        kept = {}
 
-        def row_bank():
-            return next_bank([P, CH], "h")
-
-        def quad_bank(ring_name):
-            return next_bank([P, PACK, P], ring_name)
-
-        top = {}
-
-        def stage_b(b):
-            for c in range(NCH):
-                top[b, c] = held([P, PACK, CH], F32, f"top{b}{c}")
+        def product_wa(b):
+            for half in range(S // HALF):
+                tokens = slice(half * HALF, (half + 1) * HALF)
+                kept[b, half] = held([P, PACK, HALF], F32, f"top{b}{half}")
                 for t in range(PACK):
-                    bank = row_bank()
+                    bank = next_bank([P, HALF], "h")
                     r0 = b * PASS + t * P
                     nc.tensor.matmul_mx(
                         bank[:],
                         lhsT=wa_w[:, 2 * r0 : 2 * (r0 + P)].bitcast(FP4X4),
                         lhsT_scale=wa_sc[:, r0 : r0 + P],
-                        rhs=xs_w[:, cols(c)].bitcast(FP8X4),
-                        rhs_scale=xs_sc[:, cols(c)],
+                        rhs=xs_w[:, tokens].bitcast(FP8X4),
+                        rhs_scale=xs_sc[:, tokens],
                         start=True, stop=True,
                     )
-                    nc.scalar.copy(top[b, c][:, t, :], bank[:])
+                    nc.scalar.copy(kept[b, half][:, t, :], bank[:])
 
-        stage_b(0)
-        v_w = [held([P, S], U32, f"v_w{a}") for a in range(KP)]
+        picked_sc = held([P, S], U8, "picked_sc")
+        nc.vector.tensor_copy(picked_sc[:], tab_sc[:].indirect(offsets[:]))
 
-        def round_weight(raw, copies):
+        def plane_start(a):
+            return 4 * (a + 1)
+
+        def place_scale_rows(a):
+            for r in range(4):
+                first = 64 * a + 4 * r
+                nc.sync.dma_start(
+                    v_sc[plane_start(a) + r : P : 32, :].bitcast(I32),
+                    picked_sc[first : first + 3 * 16 + 1 : 16, :].bitcast(I32),
+                )
+
+        place_scale_rows(0)
+        w1_raw[1, 0] = load_weight(w1, 1, 0, "tab_sc")
+        place_scale_rows(1)
+        product_wa(0)
+        v_w = [held([P, S], U32, f"v_w{a}") for a in range(K_PASSES)]
+
+        def gather_words(a):
+            nc.vector.tensor_copy(v_w[a][:], tab_w[a][:].bitcast(U32).indirect(offsets[:]))
+
+        def round_weight(raw, copies, pool=ring, slot="w_bf"):
             parts = len(copies)
             dealt = raw[:].rearrange("p j (m u v) -> p u m j v", u=2, v=2)
             rounded = []
             for i, copy in enumerate(copies):
-                tile = ring.tile([P, PACK * PASS // parts], BF16, name="w_bf", align_bytes=64)
+                tile = pool.tile([P, PACK * PASS // parts], BF16, name=slot, align_bytes=64)
                 us = slice(i * 2 // parts, (i + 1) * 2 // parts)
                 copy(tile[:].rearrange("p (u v m j) -> p u m j v", v=2, m=P, j=PACK), dealt[:, us, :, :, :])
                 rounded.append(tile)
@@ -171,117 +170,129 @@ def tile_list_groove_fill_features_kernel(
                     slices.append((codes[:, m0 : m0 + P].bitcast(FP8X4), scales[:, m0 : m0 + P]))
             return slices
 
-        vec, act = nc.vector.tensor_copy, nc.scalar.copy
+        on_vector, on_scalar = nc.vector.tensor_copy, nc.scalar.copy
         w1_q, wb_q = {}, {}
 
         def stage_max(b, s0, width, ts=range(PACK)):
-            tok = slice(s0, s0 + width)
-            c, at = divmod(s0, CH)
+            tokens = slice(s0, s0 + width)
+            half, at = divmod(s0, HALF)
             for t in ts:
-                bank = row_bank()
-                for a in range(KP):
+                bank = next_bank([P, HALF], "h")
+                for a in range(K_PASSES):
                     codes, scales = w1_q[a, b][t]
                     nc.tensor.matmul_mx(
                         bank[:, :width],
                         lhsT=codes,
                         lhsT_scale=scales,
-                        rhs=v_w[a][:, tok].bitcast(FP8X4),
-                        rhs_scale=v_sc[4 * (a + 1) : P, tok],
-                        start=(a == 0), stop=(a == KP - 1),
+                        rhs=v_w[a][:, tokens].bitcast(FP8X4),
+                        rhs_scale=v_sc[plane_start(a) : P, tokens],
+                        start=(a == 0), stop=(a == K_PASSES - 1),
                     )
-                kept = top[b, c][:, t, at : at + width]
-                nc.vector.scalar_tensor_tensor(kept, bank[:, :width], bias[:, b, t : t + 1], kept, ADD, MAX)
+                rows = kept[b, half][:, t, at : at + width]
+                nc.vector.scalar_tensor_tensor(rows, bank[:, :width], bias[:, b, t : t + 1], rows, ADD, MAX)
 
         def h_tile(width):
             return ring.tile([P, PACK * width], BF16, name="h_bf", align_bytes=64)
 
+        def woven(rounded, g):
+            return rounded[:, g * PASS : (g + 1) * PASS].rearrange("p (n i t) -> p n t i", i=2, t=PACK)
+
+        def in_pairs(slices):
+            return slices.rearrange("p t (n i) -> p n t i", i=2)
+
         def stage_add(b, s0, rounded, gs):
             for g in gs:
-                tok = slice(s0 + g * P, s0 + (g + 1) * P)
-                c, at = divmod(tok.start, CH)
-                bank = quad_bank("h")
+                tokens = slice(s0 + g * P, s0 + (g + 1) * P)
+                half, at = divmod(tokens.start, HALF)
+                bank = next_bank([P, PACK, P], "h")
                 for t in range(PACK):
                     codes, scales = wb_q[b][t]
                     nc.tensor.matmul_mx(
                         bank[:, t, :],
                         lhsT=codes,
                         lhsT_scale=scales,
-                        rhs=xs_w[:, tok].bitcast(FP8X4),
-                        rhs_scale=xs_sc[:, tok],
+                        rhs=xs_w[:, tokens].bitcast(FP8X4),
+                        rhs_scale=xs_sc[:, tokens],
                         start=True, stop=True,
                     )
-                kept = top[b, c][:, :, at : at + P]
-                part = rounded[:, g * PASS : (g + 1) * PASS]
                 nc.vector.tensor_tensor(
-                    part.rearrange("p (n i t) -> p n t i", i=2, t=PACK),
-                    bank[:].rearrange("p t (n i) -> p n t i", i=2),
-                    kept.rearrange("p t (n i) -> p n t i", i=2),
-                    ADD,
+                    woven(rounded, g), in_pairs(bank[:]), in_pairs(kept[b, half][:, :, at : at + P]), ADD
                 )
 
-        w2_w = held([P, HB, N], I32, "w2_w")
-        h_w = [held([P, S], U32, f"h_w{b}") for b in range(HB)]
-        h_sc = [held([P, S], U8, f"h_sc{b}") for b in range(HB)]
+        w2_w = held([P, H_BLOCKS, N], I32, "w2_w")
+        h_w = [held([P, S], U32, f"h_w{b}") for b in range(H_BLOCKS)]
+        h_sc = [held([P, S], U8, f"h_sc{b}") for b in range(H_BLOCKS)]
         y_w = held([P, S], U32, "y_w")
         y_sc = held([P, S], U8, "y_sc")
         y_rows = out_0.rearrange("(p t) s -> p t s", t=PACK)
 
         def quantise_h(b, s0, width, rounded):
-            tok = slice(s0, s0 + width)
-            nc.vector.quantize_mx(h_w[b][:, tok].bitcast(FP8X4), h_sc[b][:, tok], rounded[:])
+            tokens = slice(s0, s0 + width)
+            nc.vector.quantize_mx(h_w[b][:, tokens].bitcast(FP8X4), h_sc[b][:, tokens], rounded[:])
 
-        def stage_y(s0, width, copy):
+        def stage_y(s0, width, round_copy):
             y = ring.tile([P, PACK, width], F32, name="y", align_bytes=64)
             rounded = ring.tile([P, PACK * width], BF16, name="y_bf", align_bytes=64)
             for g in range(width // P):
-                tok = slice(s0 + g * P, s0 + (g + 1) * P)
-                bank = quad_bank("y")
-                for b in range(HB):
+                tokens = slice(s0 + g * P, s0 + (g + 1) * P)
+                bank = next_bank([P, PACK, P], "y")
+                for b in range(H_BLOCKS):
                     for t in range(PACK):
                         nc.tensor.matmul_mx(
                             bank[:, t, :],
                             lhsT=w2_w[:, b, t * P : (t + 1) * P].bitcast(FP8X4),
                             lhsT_scale=w2_sc[4 * b : P, t * P : (t + 1) * P],
-                            rhs=h_w[b][:, tok].bitcast(FP8X4),
-                            rhs_scale=h_sc[b][:, tok],
-                            start=(b == 0 and t == 0), stop=(b == HB - 1 and t == PACK - 1),
+                            rhs=h_w[b][:, tokens].bitcast(FP8X4),
+                            rhs_scale=h_sc[b][:, tokens],
+                            start=(b == 0 and t == 0), stop=(b == H_BLOCKS - 1 and t == PACK - 1),
                         )
-                copy(
-                    rounded[:, g * PASS : (g + 1) * PASS].rearrange("p (n i t) -> p n t i", i=2, t=PACK),
-                    bank[:].rearrange("p t (n i) -> p n t i", i=2),
-                )
+                round_copy(woven(rounded, g), in_pairs(bank[:]))
                 nc.scalar.copy(y[:, :, g * P : (g + 1) * P], bank[:])
             nc.sync.dma_start(y_rows[:, :, s0 : s0 + width], y[:])
             return rounded
 
-        def planes_y(s0, width, rounded):
-            tok = slice(s0, s0 + width)
-            nc.vector.quantize_mx(y_w[:, tok].bitcast(FP8X4), y_sc[:, tok], rounded[:])
-            nc.sync.dma_start(as_words(out_1[0])[:, tok], y_w[:, tok].bitcast(I32))
+        def quantise_y(s0, width, rounded):
+            tokens = slice(s0, s0 + width)
+            nc.vector.quantize_mx(y_w[:, tokens].bitcast(FP8X4), y_sc[:, tokens], rounded[:])
+            nc.sync.dma_start(as_words(out_1[0])[:, tokens], y_w[:, tokens].bitcast(I32))
 
-        nc.vector.tensor_copy(v_w[0][:], tab_w[0][:].bitcast(U32).indirect(offsets[:]))
-        w1_q[0, 0] = quantise_weight(round_weight(w1_raw[0, 0], (vec,)), "w1q00")
-        nc.vector.tensor_copy(v_sc[:], tab_sc[:].indirect(offsets[:]))
-        nc.vector.tensor_copy(v_w[1][:], tab_w[1][:].bitcast(U32).indirect(offsets[:]))
-        w1_q[1, 0] = quantise_weight(round_weight(w1_raw[1, 0], (vec, act)), "w1q10")
-        stage_b(1)
-        stage_max(0, 0, CH)
-        rounded = round_weight(wb_raw[0], (act,))
-        stage_max(0, CH, CH, range(2))
+        gather_words(0)
+        wb_raw[0] = load_weight(wb, 0, 0, "tab_w0")
+        w1_q[0, 0] = quantise_weight(round_weight(w1_raw[0, 0], (on_vector,), keep, "first_bf"), "w1q00")
+        w1_raw[0, 1] = load_weight(w1, 0, 1, "w1_raw00")
+        w1_raw[1, 1] = load_weight(w1, 1, 1, "picked_sc")
+        gather_words(1)
+        wb_raw[1] = load_weight(wb, 0, 1, "tab_w1")
+        w1_q[1, 0] = quantise_weight(round_weight(w1_raw[1, 0], (on_vector, on_scalar)), "w1q10")
+        w2_sc_raw = held([P, N], U8, "first_bf")
+        nc.vector.memset(w2_sc_raw[:].bitcast(I32), 0)
+        for quadrant in range(4):
+            nc.sync.dma_start(
+                w2_sc_raw[32 * quadrant : 32 * quadrant + 8, :].bitcast(I32),
+                w2_scales[:, 4 * quadrant : 4 * quadrant + 4, :].bitcast(I32),
+            )
+        w2_raw = held([P, H_BLOCKS, N], I32, "tab_sc")
+        nc.sync.dma_start(w2_raw[:], w2_words.rearrange("a p n t -> p a (n t)").bitcast(I32))
+        product_wa(1)
+
+        stage_max(0, 0, HALF)
+        rounded = round_weight(wb_raw[0], (on_scalar,))
+        stage_max(0, HALF, HALF, range(2))
         wb_q[0] = quantise_weight(rounded, "wbq0")
-        stage_max(0, CH, CH, range(2, 4))
-        rounded = round_weight(w1_raw[0, 1], (act,))
-        h00 = h_tile(CH)
-        stage_add(0, 0, h00, range(2))
+        stage_max(0, HALF, HALF, range(2, PACK))
+        rounded = round_weight(w1_raw[0, 1], (on_scalar,))
+        h_first = h_tile(HALF)
+        stage_add(0, 0, h_first, range(2))
         w1_q[0, 1] = quantise_weight(rounded, "w1q01")
-        rounded = round_weight(w1_raw[1, 1], (act,))
-        stage_add(0, 0, h00, range(2, 4))
+        rounded = round_weight(w1_raw[1, 1], (on_scalar,))
+        stage_add(0, 0, h_first, range(2, HALF // P))
         w1_q[1, 1] = quantise_weight(rounded, "w1q11")
-        quantise_h(0, 0, CH, h00)
-        rounded = round_weight(wb_raw[1], (act,))
-        stage_max(1, 0, CH, range(3))
+        quantise_h(0, 0, HALF, h_first)
+        rounded = round_weight(wb_raw[1], (on_scalar,))
+        stage_max(1, 0, HALF, range(PACK - 1))
         wb_q[1] = quantise_weight(rounded, "wbq1")
-        stage_max(1, 0, CH, range(3, 4))
+        stage_max(1, 0, HALF, range(PACK - 1, PACK))
+
         w2_sc = held([P, N], U8, "w2_sc")
         nc.gpsimd.tensor_copy(
             w2_sc[:].rearrange("p (t m) -> p t m", t=PACK),
@@ -291,40 +302,41 @@ def tile_list_groove_fill_features_kernel(
             w2_w[:].bitcast(U32).rearrange("p a (u v m) -> p a u m v", u=2, v=2),
             w2_raw[:].bitcast(U32).rearrange("p a (m u v) -> p a u m v", u=2, v=2),
         )
-        wide = 2 * P
-        pieces = [(s0, wide) for s0 in range(0, S - wide, wide)] + [(S - wide, P), (S - P, P)]
-        first, second = pieces[:2], pieces[2:]
+
+        pieces = [(s0, QUARTER) for s0 in range(0, S - QUARTER, QUARTER)] + [(S - QUARTER, P), (S - P, P)]
+        first_half, third_quarter, last_two = pieces[:2], pieces[2], pieces[3:]
         h_bf, y_bf = {}, {}
 
         def add_piece(piece):
-            h_bf[piece] = h_tile(piece[1])
-            stage_add(1, piece[0], h_bf[piece], range(piece[1] // P))
+            s0, width = piece
+            h_bf[piece] = h_tile(width)
+            stage_add(1, s0, h_bf[piece], range(width // P))
 
-        for piece in first:
+        for piece in first_half:
             add_piece(piece)
-        for piece in first:
+        for piece in first_half:
             quantise_h(1, *piece, h_bf[piece])
-        for piece in first:
-            y_bf[piece] = stage_y(*piece, act)
-        h01 = h_tile(CH)
-        stage_add(0, CH, h01, range(CH // P))
-        planes_y(*first[0], y_bf[first[0]])
-        stage_max(1, CH, wide)
-        quantise_h(0, CH, CH, h01)
-        add_piece(second[0])
-        planes_y(*first[1], y_bf[first[1]])
-        quantise_h(1, *second[0], h_bf[second[0]])
-        y_bf[second[0]] = stage_y(*second[0], act)
-        stage_max(1, CH + wide, wide)
-        for piece in second[1:]:
+        for piece in first_half:
+            y_bf[piece] = stage_y(*piece, on_scalar)
+        h_second = h_tile(HALF)
+        stage_add(0, HALF, h_second, range(HALF // P))
+        quantise_y(*first_half[0], y_bf[first_half[0]])
+        stage_max(1, *third_quarter)
+        quantise_h(0, HALF, HALF, h_second)
+        add_piece(third_quarter)
+        quantise_y(*first_half[1], y_bf[first_half[1]])
+        quantise_h(1, *third_quarter, h_bf[third_quarter])
+        y_bf[third_quarter] = stage_y(*third_quarter, on_scalar)
+        stage_max(1, S - QUARTER, QUARTER)
+        for piece in last_two:
             add_piece(piece)
-        planes_y(*second[0], y_bf[second[0]])
-        for piece in second[1:]:
+        quantise_y(*third_quarter, y_bf[third_quarter])
+        for piece in last_two:
             quantise_h(1, *piece, h_bf[piece])
-        y_bf[second[1]] = stage_y(*second[1], act)
-        y_bf[second[2]] = stage_y(*second[2], vec)
-        for piece in second[1:]:
-            planes_y(*piece, y_bf[piece])
-        for q in range(4):
-            queue = nc.scalar if q % 2 else nc.sync
-            queue.dma_start(out_2[0, q:16:4, :].bitcast(I32), y_sc[q:P:32, :].bitcast(I32))
+        for piece, round_copy in zip(last_two, (on_scalar, on_vector)):
+            y_bf[piece] = stage_y(*piece, round_copy)
+        for piece in last_two:
+            quantise_y(*piece, y_bf[piece])
+        for r in range(4):
+            queue = nc.scalar if r % 2 else nc.sync
+            queue.dma_start(out_2[0, r:16:4, :].bitcast(I32), y_sc[r:P:32, :].bitcast(I32))

from contextlib import ExitStack

import concourse.mybir as mybir

K, T, S, K2, H, N = 1024, 4096, 1024, 512, 1024, 512
FLOPS = 2 * S * (K * H + 2 * K2 * H + H * N)

F32 = mybir.dt.float32
BF16 = mybir.dt.bfloat16
I32 = mybir.dt.int32
U32 = mybir.dt.uint32
U16 = mybir.dt.uint16
U8 = mybir.dt.uint8
FP8X4 = mybir.dt.float8_e4m3fn_x4
FP4X4 = mybir.dt.float4_e2m1fn_x4
ADD = mybir.AluOpType.add
MAX = mybir.AluOpType.max

P = 128
PACK = 4
PASS = P * PACK
K_PASSES = K // PASS
H_BLOCKS = H // PASS
HALF = 512
QUARTER = HALF // 2
RING_DEPTH = 4
BANKS = {"h": 5, "y": 3}


def tile_list_groove_fill_features_kernel(
    tc, tab_words, tab_scales, offs, xs_words, xs_scales, w1, b1, wa_words, wa_scales, wb,
    w2_words, w2_scales, out_0, out_1, out_2,
):
    nc = tc.nc
    with ExitStack() as ctx:
        keep = ctx.enter_context(tc.tile_pool(name="keep", bufs=1))
        ring = ctx.enter_context(tc.tile_pool(name="ring", bufs=RING_DEPTH))
        psum = ctx.enter_context(tc.psum_pool(name="psum", bufs=1))

        def held(shape, dtype, slot):
            return keep.tile(shape, dtype, name=slot, align_bytes=64)

        def as_words(dram):
            return dram.rearrange("p n t -> p (n t)").bitcast(I32)

        offsets = keep.tile([P, S // 16], U16, name="offsets")
        tab_sc = held([P, T], U8, "tab_sc")
        xs_sc = held([P, S], U8, "xs_sc")
        wa_sc_raw = held([P, H], U8, "wa_sc_raw")
        v_sc = held([P, S], U8, "v_sc")
        for plane in (wa_sc_raw, tab_sc, xs_sc, v_sc):
            nc.vector.memset(plane[:].bitcast(I32), 0)

        def load_scale_rows(plane, dram):
            for r in range(4):
                nc.sync.dma_start(plane[r:P:32, :], dram[r:16:4, :].bitcast(I32))

        def load_weight(w, a, b, slot):
            raw = held([P, PACK, PASS], F32, slot)
            rows = w[a * PASS : (a + 1) * PASS, b * PASS : (b + 1) * PASS]
            nc.sync.dma_start(raw[:], rows.rearrange("(p j) c -> p j c", j=PACK))
            return raw

        tab_w = [held([P, T], I32, f"tab_w{a}") for a in range(K_PASSES)]

        def load_table(a, part):
            columns = slice(part * T // 2, (part + 1) * T // 2)
            nc.sync.dma_start(tab_w[a][:, columns], as_words(tab_words[a])[:, columns])

        xs_w = held([P, S], I32, "xs_w")
        nc.sync.dma_start(xs_w[:], as_words(xs_words[0]))
        wa_raw = held([P, 2 * H], U8, "wa_raw")
        nc.sync.dma_start(wa_raw[:].bitcast(I32), wa_words[0].bitcast(I32))
        xs_sc_rows = held([P, S // 4], I32, "xs_sc_rows")
        load_scale_rows(xs_sc_rows[:], xs_scales[0])
        for quadrant in range(4):
            live = slice(32 * quadrant, 32 * quadrant + 4)
            nc.vector.tensor_copy(xs_sc[live, :].bitcast(I32), xs_sc_rows[live, :])
        nc.sync.dma_start(offsets[:], offs)
        load_table(0, 0)
        load_scale_rows(wa_sc_raw[:].bitcast(I32), wa_scales[0])
        nc.sync.dma_start(tab_sc[0:P:4, :].bitcast(I32), tab_scales.rearrange("a q n -> (a q) n").bitcast(I32))
        load_table(0, 1)
        w1_raw, wb_raw = {}, {}
        w1_raw[0, 0] = load_weight(w1, 0, 0, "w1_raw00")
        load_table(1, 0)
        load_table(1, 1)
        bias = held([P, H_BLOCKS, PACK], F32, "bias")
        nc.sync.dma_start(bias[:], b1.rearrange("(b p t) -> p b t", p=P, t=PACK))

        wa_w = held([P, 2 * H], U8, "wa_w")
        wa_sc = held([P, H], U8, "wa_sc")
        nc.vector.tensor_copy(
            wa_w[:].bitcast(U16).rearrange("p (b t m) -> p b t m", b=H_BLOCKS, t=PACK),
            wa_raw[:].bitcast(U16).rearrange("p (b m t) -> p b t m", b=H_BLOCKS, t=PACK),
        )
        nc.vector.tensor_copy(
            wa_sc[:].rearrange("p (b t m) -> p b t m", b=H_BLOCKS, t=PACK),
            wa_sc_raw[:].rearrange("p (b m t) -> p b t m", b=H_BLOCKS, t=PACK),
        )

        banks_taken = {"h": [], "y": []}

        def next_bank(shape, use):
            taken = banks_taken[use]
            taken.append(psum.tile(shape, F32, name=f"{use}_bank{len(taken) % BANKS[use]}"))
            return taken[-1]

        kept = {}

        def product_wa(b):
            for half in range(S // HALF):
                tokens = slice(half * HALF, (half + 1) * HALF)
                kept[b, half] = held([P, PACK, HALF], F32, f"top{b}{half}")
                for t in range(PACK):
                    bank = next_bank([P, HALF], "h")
                    r0 = b * PASS + t * P
                    nc.tensor.matmul_mx(
                        bank[:],
                        lhsT=wa_w[:, 2 * r0 : 2 * (r0 + P)].bitcast(FP4X4),
                        lhsT_scale=wa_sc[:, r0 : r0 + P],
                        rhs=xs_w[:, tokens].bitcast(FP8X4),
                        rhs_scale=xs_sc[:, tokens],
                        start=True, stop=True,
                    )
                    nc.scalar.copy(kept[b, half][:, t, :], bank[:])

        picked_sc = held([P, S], U8, "picked_sc")
        nc.vector.tensor_copy(picked_sc[:], tab_sc[:].indirect(offsets[:]))

        def plane_start(a):
            return 4 * (a + 1)

        def place_scale_rows(a):
            for r in range(4):
                first = 64 * a + 4 * r
                nc.sync.dma_start(
                    v_sc[plane_start(a) + r : P : 32, :].bitcast(I32),
                    picked_sc[first : first + 3 * 16 + 1 : 16, :].bitcast(I32),
                )

        place_scale_rows(0)
        w1_raw[1, 0] = load_weight(w1, 1, 0, "tab_sc")
        place_scale_rows(1)
        product_wa(0)
        v_w = [held([P, S], U32, f"v_w{a}") for a in range(K_PASSES)]

        def gather_words(a):
            nc.vector.tensor_copy(v_w[a][:], tab_w[a][:].bitcast(U32).indirect(offsets[:]))

        def round_weight(raw, copies, pool=ring, slot="w_bf"):
            parts = len(copies)
            dealt = raw[:].rearrange("p j (m u v) -> p u m j v", u=2, v=2)
            rounded = []
            for i, copy in enumerate(copies):
                tile = pool.tile([P, PACK * PASS // parts], BF16, name=slot, align_bytes=64)
                us = slice(i * 2 // parts, (i + 1) * 2 // parts)
                copy(tile[:].rearrange("p (u v m j) -> p u m j v", v=2, m=P, j=PACK), dealt[:, us, :, :, :])
                rounded.append(tile)
            return rounded

        def quantise_weight(rounded, name):
            slices = []
            for i, tile in enumerate(rounded):
                width = tile.shape[1] // PACK
                codes = held([P, width], U32, f"{name}{i}_w")
                scales = held([P, width], U8, f"{name}{i}_sc")
                nc.vector.quantize_mx(codes[:].bitcast(FP8X4), scales[:], tile[:])
                for m0 in range(0, width, P):
                    slices.append((codes[:, m0 : m0 + P].bitcast(FP8X4), scales[:, m0 : m0 + P]))
            return slices

        on_vector, on_scalar = nc.vector.tensor_copy, nc.scalar.copy
        w1_q, wb_q = {}, {}

        def stage_max(b, s0, width, ts=range(PACK)):
            tokens = slice(s0, s0 + width)
            half, at = divmod(s0, HALF)
            for t in ts:
                bank = next_bank([P, HALF], "h")
                for a in range(K_PASSES):
                    codes, scales = w1_q[a, b][t]
                    nc.tensor.matmul_mx(
                        bank[:, :width],
                        lhsT=codes,
                        lhsT_scale=scales,
                        rhs=v_w[a][:, tokens].bitcast(FP8X4),
                        rhs_scale=v_sc[plane_start(a) : P, tokens],
                        start=(a == 0), stop=(a == K_PASSES - 1),
                    )
                rows = kept[b, half][:, t, at : at + width]
                nc.vector.scalar_tensor_tensor(rows, bank[:, :width], bias[:, b, t : t + 1], rows, ADD, MAX)

        def h_tile(width):
            return ring.tile([P, PACK * width], BF16, name="h_bf", align_bytes=64)

        def woven(rounded, g):
            return rounded[:, g * PASS : (g + 1) * PASS].rearrange("p (n i t) -> p n t i", i=2, t=PACK)

        def in_pairs(slices):
            return slices.rearrange("p t (n i) -> p n t i", i=2)

        def stage_add(b, s0, rounded, gs):
            for g in gs:
                tokens = slice(s0 + g * P, s0 + (g + 1) * P)
                half, at = divmod(tokens.start, HALF)
                bank = next_bank([P, PACK, P], "h")
                for t in range(PACK):
                    codes, scales = wb_q[b][t]
                    nc.tensor.matmul_mx(
                        bank[:, t, :],
                        lhsT=codes,
                        lhsT_scale=scales,
                        rhs=xs_w[:, tokens].bitcast(FP8X4),
                        rhs_scale=xs_sc[:, tokens],
                        start=True, stop=True,
                    )
                nc.vector.tensor_tensor(
                    woven(rounded, g), in_pairs(bank[:]), in_pairs(kept[b, half][:, :, at : at + P]), ADD
                )

        w2_w = held([P, H_BLOCKS, N], I32, "w2_w")
        h_w = [held([P, S], U32, f"h_w{b}") for b in range(H_BLOCKS)]
        h_sc = [held([P, S], U8, f"h_sc{b}") for b in range(H_BLOCKS)]
        y_w = held([P, S], U32, "y_w")
        y_sc = held([P, S], U8, "y_sc")
        y_rows = out_0.rearrange("(p t) s -> p t s", t=PACK)

        def quantise_h(b, s0, width, rounded):
            tokens = slice(s0, s0 + width)
            nc.vector.quantize_mx(h_w[b][:, tokens].bitcast(FP8X4), h_sc[b][:, tokens], rounded[:])

        def stage_y(s0, width, round_copy):
            y = ring.tile([P, PACK, width], F32, name="y", align_bytes=64)
            rounded = ring.tile([P, PACK * width], BF16, name="y_bf", align_bytes=64)
            for g in range(width // P):
                tokens = slice(s0 + g * P, s0 + (g + 1) * P)
                bank = next_bank([P, PACK, P], "y")
                for b in range(H_BLOCKS):
                    for t in range(PACK):
                        nc.tensor.matmul_mx(
                            bank[:, t, :],
                            lhsT=w2_w[:, b, t * P : (t + 1) * P].bitcast(FP8X4),
                            lhsT_scale=w2_sc[4 * b : P, t * P : (t + 1) * P],
                            rhs=h_w[b][:, tokens].bitcast(FP8X4),
                            rhs_scale=h_sc[b][:, tokens],
                            start=(b == 0 and t == 0), stop=(b == H_BLOCKS - 1 and t == PACK - 1),
                        )
                round_copy(woven(rounded, g), in_pairs(bank[:]))
                nc.scalar.copy(y[:, :, g * P : (g + 1) * P], bank[:])
            nc.sync.dma_start(y_rows[:, :, s0 : s0 + width], y[:])
            return rounded

        def quantise_y(s0, width, rounded):
            tokens = slice(s0, s0 + width)
            nc.vector.quantize_mx(y_w[:, tokens].bitcast(FP8X4), y_sc[:, tokens], rounded[:])
            nc.sync.dma_start(as_words(out_1[0])[:, tokens], y_w[:, tokens].bitcast(I32))

        gather_words(0)
        wb_raw[0] = load_weight(wb, 0, 0, "tab_w0")
        w1_q[0, 0] = quantise_weight(round_weight(w1_raw[0, 0], (on_vector,), keep, "first_bf"), "w1q00")
        w1_raw[0, 1] = load_weight(w1, 0, 1, "w1_raw00")
        w1_raw[1, 1] = load_weight(w1, 1, 1, "picked_sc")
        gather_words(1)
        wb_raw[1] = load_weight(wb, 0, 1, "tab_w1")
        w1_q[1, 0] = quantise_weight(round_weight(w1_raw[1, 0], (on_vector, on_scalar)), "w1q10")
        w2_sc_raw = held([P, N], U8, "first_bf")
        nc.vector.memset(w2_sc_raw[:].bitcast(I32), 0)
        for quadrant in range(4):
            nc.sync.dma_start(
                w2_sc_raw[32 * quadrant : 32 * quadrant + 8, :].bitcast(I32),
                w2_scales[:, 4 * quadrant : 4 * quadrant + 4, :].bitcast(I32),
            )
        w2_raw = held([P, H_BLOCKS, N], I32, "tab_sc")
        nc.sync.dma_start(w2_raw[:], w2_words.rearrange("a p n t -> p a (n t)").bitcast(I32))
        product_wa(1)

        stage_max(0, 0, HALF)
        rounded = round_weight(wb_raw[0], (on_scalar,))
        stage_max(0, HALF, HALF, range(2))
        wb_q[0] = quantise_weight(rounded, "wbq0")
        stage_max(0, HALF, HALF, range(2, PACK))
        rounded = round_weight(w1_raw[0, 1], (on_scalar,))
        h_first = h_tile(HALF)
        stage_add(0, 0, h_first, range(2))
        w1_q[0, 1] = quantise_weight(rounded, "w1q01")
        rounded = round_weight(w1_raw[1, 1], (on_scalar,))
        stage_add(0, 0, h_first, range(2, HALF // P))
        w1_q[1, 1] = quantise_weight(rounded, "w1q11")
        quantise_h(0, 0, HALF, h_first)
        rounded = round_weight(wb_raw[1], (on_scalar,))
        stage_max(1, 0, HALF, range(PACK - 1))
        wb_q[1] = quantise_weight(rounded, "wbq1")
        stage_max(1, 0, HALF, range(PACK - 1, PACK))

        w2_sc = held([P, N], U8, "w2_sc")
        nc.gpsimd.tensor_copy(
            w2_sc[:].rearrange("p (t m) -> p t m", t=PACK),
            w2_sc_raw[:].rearrange("p (m t) -> p t m", t=PACK),
        )
        nc.scalar.copy(
            w2_w[:].bitcast(U32).rearrange("p a (u v m) -> p a u m v", u=2, v=2),
            w2_raw[:].bitcast(U32).rearrange("p a (m u v) -> p a u m v", u=2, v=2),
        )

        pieces = [(s0, QUARTER) for s0 in range(0, S - QUARTER, QUARTER)] + [(S - QUARTER, P), (S - P, P)]
        first_half, third_quarter, last_two = pieces[:2], pieces[2], pieces[3:]
        h_bf, y_bf = {}, {}

        def add_piece(piece):
            s0, width = piece
            h_bf[piece] = h_tile(width)
            stage_add(1, s0, h_bf[piece], range(width // P))

        for piece in first_half:
            add_piece(piece)
        for piece in first_half:
            quantise_h(1, *piece, h_bf[piece])
        for piece in first_half:
            y_bf[piece] = stage_y(*piece, on_scalar)
        h_second = h_tile(HALF)
        stage_add(0, HALF, h_second, range(HALF // P))
        quantise_y(*first_half[0], y_bf[first_half[0]])
        stage_max(1, *third_quarter)
        quantise_h(0, HALF, HALF, h_second)
        add_piece(third_quarter)
        quantise_y(*first_half[1], y_bf[first_half[1]])
        quantise_h(1, *third_quarter, h_bf[third_quarter])
        y_bf[third_quarter] = stage_y(*third_quarter, on_scalar)
        stage_max(1, S - QUARTER, QUARTER)
        for piece in last_two:
            add_piece(piece)
        quantise_y(*third_quarter, y_bf[third_quarter])
        for piece in last_two:
            quantise_h(1, *piece, h_bf[piece])
        for piece, round_copy in zip(last_two, (on_scalar, on_vector)):
            y_bf[piece] = stage_y(*piece, round_copy)
        for piece in last_two:
            quantise_y(*piece, y_bf[piece])
        for r in range(4):
            queue = nc.scalar if r % 2 else nc.sync
            queue.dma_start(out_2[0, r:16:4, :].bitcast(I32), y_sc[r:P:32, :].bitcast(I32))
